import numpy as np
import ml_dtypes


def mxq(x, axis, fmt="e4m3"):
    dtype, down = {"e4m3": (ml_dtypes.float8_e4m3fn, 7), "e5m2": (ml_dtypes.float8_e5m2, 14)}[fmt]
    v = np.moveaxis(np.asarray(x, np.float32).astype(ml_dtypes.bfloat16).astype(np.float64), axis, -1)
    blocks = v.reshape(v.shape[:-1] + (-1, 32))
    amax = np.abs(blocks).max(-1, keepdims=True)
    byte = np.maximum(np.where(amax > 0, np.frexp(amax)[1] - 1 + 127, 0) - down, 1)
    scale = np.exp2(byte - 127.0)
    codes = (blocks / scale).astype(np.float32).astype(dtype).astype(np.float64)
    return np.moveaxis((codes * scale).reshape(v.shape), -1, axis)


WIDE = False


def mx_kscale(k):
    if not WIDE:
        return np.ones(k)
    levels = np.array([10, -10, 5, -5, 0])
    if k % 512:
        return np.exp2(np.random.permutation(np.resize(levels, k // 32))).repeat(32)
    a = np.empty((k // 512, 16))
    for p in range(k // 512):
        a[p, :8] = np.random.permutation(np.resize(levels, 8))
        for g in range(8):
            far = levels[np.abs(levels - a[p, g]) >= 10]
            a[p, g + 8] = far[np.random.randint(len(far))]
    return np.exp2(a.ravel()).repeat(32)


def f64(x):
    return np.asarray(x).astype(np.float64)


def striped(idx):
    return np.tile(idx.reshape(-1, 16).T, (8, 1)).astype(np.uint16)


def unstriped(offs):
    return offs[:16].T.reshape(-1).astype(np.int64)


def striped8(idx):
    return np.concatenate([x.reshape(-1, 16).T for x in idx]).astype(np.uint16)


def runs(offs, k):
    lists = np.stack([offs[16 * r : 16 * r + 16].T.reshape(-1) for r in range(8)]).astype(np.int64)
    return lists[np.arange(k) % 512 // 64]


def pack_weight(w):
    k, n = w.shape
    w = f64(np.asarray(w, np.float32).astype(ml_dtypes.bfloat16)).reshape(k // 32, 32, n)
    amax = np.abs(w).max(1)
    byte = np.clip(np.where(amax > 0, np.frexp(amax)[1] - 1 + 127 - 7, 1), 1, 254)
    scaled = (w * np.exp2(127.0 - byte)[:, None, :]).reshape(k, n).astype(np.float32)
    words = np.ascontiguousarray(scaled.reshape(k // 512, 128, 4, n).transpose(0, 1, 3, 2)).astype(ml_dtypes.float8_e4m3fn).view(np.uint8)
    return words, np.ascontiguousarray(byte.astype(np.uint8).reshape(k // 512, 16, n))


def unpack_weight(words, scales):
    g, p, n, _ = words.shape
    vals = np.ascontiguousarray(words).view(ml_dtypes.float8_e4m3fn).astype(np.float64) * np.repeat(np.exp2(scales.astype(np.float64) - 127.0), 8, axis=1)[..., None]
    return vals.transpose(0, 1, 3, 2).reshape(g * 512, n)


def sigmoid(v):
    return 1.0 / (1.0 + np.exp(-np.maximum(v, -700.0)))

def planes(y):
    n, m = y.shape
    v = y.astype(np.float32).astype(ml_dtypes.bfloat16).astype(np.float64).reshape(n // 32, 32, m)
    top = np.abs(v).max(1)
    byte = np.clip(np.where(top > 0, np.frexp(top)[1] - 1 + 127 - 7, 1), 1, 254)
    codes = (v * np.exp2(127.0 - byte)[:, None, :]).reshape(n, m).astype(np.float32).astype(ml_dtypes.float8_e4m3fn).view(np.uint8)
    words = codes.reshape(n // 512, 128, 4, m).transpose(0, 1, 3, 2)
    return np.ascontiguousarray(words), np.ascontiguousarray(byte.astype(np.uint8).reshape(n // 512, 16, m))


K, T, S, N, G, H = 512, 1024, 512, 512, 2048, 512


def setup_inputs():
    n = np.random.standard_normal
    s = mx_kscale(K)[:, None]
    u = mx_kscale(S)
    packed_xT = pack_weight(n((K, T)) * s)
    packed_dT = pack_weight(n((K, G)) / s)
    packed_w1 = pack_weight(n((H, N)) / np.sqrt(H) / u[:, None])
    return {
        "x_words": packed_xT[0],
        "x_scales": packed_xT[1],
        "d_words": packed_dT[0],
        "d_scales": packed_dT[1],
        "gn": (np.random.uniform(0.5, 1.5, (H, 1)) * u[:, None]).astype(np.float32),
        "w1_words": packed_w1[0],
        "w1_scales": packed_w1[1],
        "offs": striped(np.random.permutation(T)[:S]),
        "k1": striped8(np.random.randint(0, G, (8, H))),
        "two": striped(np.random.permutation(T)[:S]),
        "k2": striped8(np.random.randint(0, G, (8, H))),
        "n1": striped(np.random.permutation(S)),
        "n2": striped(np.random.permutation(S)),
        "n3": striped(np.random.randint(0, S, G)),
    }


def reference(x_words, x_scales, d_words, d_scales, gn, w1_words, w1_scales, offs, k1, two, k2, n1, n2, n3):
    d_k1 = unpack_weight(d_words, d_scales)[np.arange(K)[:, None], runs(k1, K)]
    xq = unpack_weight(x_words, x_scales)[:, unstriped(offs)]
    a = 0.0625 * (d_k1.T @ xq)
    d_k2 = unpack_weight(d_words, d_scales)[np.arange(K)[:, None], runs(k2, K)]
    x_two = unpack_weight(x_words, x_scales)[:, unstriped(two)]
    b = 0.0625 * (d_k2.T @ x_two)
    z = f64(gn) * (a * (sigmoid(b[:, unstriped(n2)])) - (0.5 * a[:, unstriped(n1)]))
    h = unpack_weight(w1_words, w1_scales).T @ mxq(z, 0, "e4m3")
    mb = h[:, unstriped(n3)]
    mx = mb.reshape(N, S, 4).max(axis=2)
    mn = mb.reshape(N, S, 4).min(axis=2)
    out_0 = np.maximum(np.minimum(1.5 * h, mx), mn)
    return (out_0,) + planes(out_0)

@@ -1,0 +1,232 @@
+from contextlib import ExitStack
+
+import concourse.mybir as mybir
+
+F32 = mybir.dt.float32
+BF16 = mybir.dt.bfloat16
+I32 = mybir.dt.int32
+U32 = mybir.dt.uint32
+U16 = mybir.dt.uint16
+U8 = mybir.dt.uint8
+FP8X4 = mybir.dt.float8_e4m3fn_x4
+ALU = mybir.AluOpType
+ACT = mybir.ActivationFunctionType
+
+P = 128
+PACK = 4
+S = 512
+TOKENS = 1024
+CODEWORDS = 2048
+MEMBERS = 4
+SPARE = 32
+HALF = S // 2
+CHUNKS = (64, 128, 128, 128, 64)
+FLOPS = 3 * 2 * 512 * 512 * 512
+
+
+def tile_picked_twpqgatebgclip_none_po_kernel(
+    tc, x_words, x_scales, d_words, d_scales, gn, w1_words, w1_scales,
+    offs, k1, two, k2, n1, n2, n3, out_0, out_1, out_2,
+):
+    nc = tc.nc
+
+    def words_of(dram):
+        return dram[0].rearrange("p n t -> p (n t)").bitcast(I32)
+
+    with ExitStack() as ctx:
+        lists = ctx.enter_context(tc.tile_pool(name="lists", bufs=1))
+        keep = ctx.enter_context(tc.tile_pool(name="keep", bufs=1))
+        ring = ctx.enter_context(tc.tile_pool(name="ring", bufs=3))
+        psum = ctx.enter_context(tc.psum_pool(name="psum", bufs=1))
+
+        def load_list(dram, name):
+            tile = lists.tile([P, dram.shape[1]], U16, name=name)
+            nc.sync.dma_start(tile[:], dram)
+            return tile
+
+        d_scale_table = keep.tile([P, CODEWORDS], U8, name="d_scale_table")
+        x_scale_table = keep.tile([P, TOKENS], U8, name="x_scale_table")
+        nc.gpsimd.memset(x_scale_table[:].bitcast(I32), 0)
+        nc.gpsimd.memset(d_scale_table[:].bitcast(I32), 0)
+
+        two_list = load_list(two, "two_list")
+        k2_list = load_list(k2, "k2_list")
+        nc.sync.dma_start(x_scale_table[0:P:8, :].bitcast(I32), x_scales[0].bitcast(I32))
+        nc.sync.dma_start(d_scale_table[0:P:8, :].bitcast(I32), d_scales[0].bitcast(I32))
+        x_word_table = keep.tile([P, TOKENS], U32, name="x_word_table")
+        nc.sync.dma_start(x_word_table[:].bitcast(I32), words_of(x_words))
+        d_word_table = keep.tile([P, CODEWORDS], U32, name="d_word_table")
+        nc.sync.dma_start(d_word_table[:].bitcast(I32), words_of(d_words))
+        k1_list = load_list(k1, "k1_list")
+        offs_list = load_list(offs, "offs_list")
+
+        w1_scale_rows = keep.tile([P, S], U8, name="w1_scale_rows")
+        nc.vector.memset(w1_scale_rows[:].bitcast(I32), 0)
+        for q in range(4):
+            nc.gpsimd.dma_start(
+                w1_scale_rows[32 * q : 32 * q + 4, :].bitcast(I32), w1_scales[0, 4 * q : 4 * q + 4, :].bitcast(I32)
+            )
+        w1_word_rows = keep.tile([P, S], U32, name="w1_word_rows")
+        nc.gpsimd.dma_start(w1_word_rows[:].bitcast(I32), words_of(w1_words))
+
+        def window(name):
+            tile = keep.tile([P, S + SPARE], F32, name=name)
+            nc.vector.memset(tile[:, S:], 0.0)
+            return tile
+
+        gate_rows = [window("gate_rows%d" % t) for t in range(PACK)]
+        h_rows = [window("h_rows%d" % t) for t in range(PACK)]
+
+        def deal(copy, dealt, plain, run):
+            copy(
+                dealt.rearrange("p (t c i) -> p c t i", t=PACK, i=run),
+                plain.rearrange("p (c i t) -> p c t i", t=PACK, i=run),
+            )
+
+        def coded_product(name, code_list, token_list, picked_tag, dealt_tag):
+            picked_scales = keep.tile([P, 2 * S], U8, name=name + "_picked_scales", tag="picked_scales")
+            placed_scales = keep.tile([P, 2 * S], U8, name=name + "_placed_scales", align_bytes=64)
+            nc.vector.memset(placed_scales[:].bitcast(I32), 0)
+            nc.vector.tensor_copy(picked_scales[:, S:], x_scale_table[:].indirect(token_list[:]))
+            nc.vector.tensor_copy(picked_scales[:, :S], d_scale_table[:].indirect(code_list[:]))
+            for r in range(4):
+                nc.sync.dma_start(
+                    placed_scales[r:P:32, :].bitcast(I32), picked_scales[8 * r : P : 32, :].bitcast(I32)
+                )
+            x_picked = keep.tile([P, S], U32, name=name + "_x_picked", tag="x_picked", align_bytes=64)
+            nc.vector.tensor_copy(x_picked[:], x_word_table[:].indirect(token_list[:]))
+            d_picked = keep.tile([P, S], U32, name=name + "_d_picked", tag=picked_tag, align_bytes=64)
+            nc.vector.tensor_copy(d_picked[:], d_word_table[:].indirect(code_list[:]))
+            d_dealt = keep.tile([P, S], U32, name=name + "_d_dealt", tag=dealt_tag, align_bytes=64)
+            deal(nc.vector.tensor_copy, d_dealt[:], d_picked[:], 4)
+            d_dealt_scales = keep.tile([P, S], U8, name=name + "_d_dealt_scales", align_bytes=64)
+            deal(nc.vector.tensor_copy, d_dealt_scales[:], placed_scales[:, :S], 16)
+            banks = []
+            for t in range(PACK):
+                cols = slice(t * P, (t + 1) * P)
+                bank = psum.tile([P, S], F32, name=name + "_bank%d" % t, tag=name + "_bank%d" % t)
+                nc.tensor.matmul_mx(
+                    bank[:],
+                    lhsT=d_dealt[:, cols].bitcast(FP8X4), lhsT_scale=d_dealt_scales[:, cols],
+                    rhs=x_picked[:].bitcast(FP8X4), rhs_scale=placed_scales[:, S:],
+                    start=True, stop=True,
+                )
+                banks.append(bank)
+            return banks
+
+        b_banks = coded_product("b", k2_list, two_list, "first_words", "second_words")
+        n2_list = load_list(n2, "n2_list")
+        gain = keep.tile([P, PACK], F32, name="gain")
+        nc.sync.dma_start(gain[:], gn.rearrange("(p t) o -> p (t o)", t=PACK))
+        n1_list = load_list(n1, "n1_list")
+        n3_list = load_list(n3, "n3_list")
+
+        w1_dealt = keep.tile([P, S], U32, name="w1_dealt", align_bytes=64)
+        deal(nc.gpsimd.tensor_copy, w1_dealt[:], w1_word_rows[:], 4)
+        w1_dealt_scales = keep.tile([P, S], U8, name="w1_dealt_scales", align_bytes=64)
+        deal(nc.gpsimd.tensor_copy, w1_dealt_scales[:], w1_scale_rows[:], 16)
+
+        gate = keep.tile([P, PACK, S], F32, name="gate")
+        for t in range(PACK):
+            nc.scalar.activation(gate_rows[t][:, :S], b_banks[t][:], ACT.Sigmoid, scale=0.0625)
+            nc.scalar.activation(gate[:, t, :], gate_rows[t][:].indirect(n2_list[:]), ACT.Copy)
+
+        a_banks = coded_product("a", k1_list, offs_list, "second_words", "first_words")
+
+        gain_a = keep.tile([P, PACK], F32, name="gain_a")
+        gain_half = keep.tile([P, PACK], F32, name="gain_half")
+        nc.vector.tensor_scalar(gain_a[:], gain[:], 0.0625, None, ALU.mult)
+        nc.vector.tensor_scalar(gain_half[:], gain[:], -0.03125, None, ALU.mult)
+
+        half_rows = [keep.tile([P, S], F32, name="half_rows%d" % t) for t in range(PACK)]
+        for t in range(PACK):
+            nc.vector.tensor_scalar(half_rows[t][:], a_banks[t][:], gain_half[:, t : t + 1], None, ALU.mult)
+        gated = keep.tile([P, PACK, S], F32, name="gated")
+        for t in range(PACK):
+            nc.vector.scalar_tensor_tensor(
+                gated[:, t, :], a_banks[t][:], gain_a[:, t : t + 1], gate[:, t, :], ALU.mult, ALU.mult
+            )
+
+        h_banks = {}
+        for half in range(2):
+            cols = slice(half * HALF, (half + 1) * HALF)
+            fetched = keep.tile([P, PACK, HALF], F32, name="fetched%d" % half)
+            for t in range(PACK):
+                looked_up = half_rows[t][:].indirect(n1_list[:, half * HALF // 16 : (half + 1) * HALF // 16])
+                if half == 1 and t == PACK - 1:
+                    nc.vector.tensor_copy(fetched[:, t, :], looked_up)
+                else:
+                    nc.scalar.activation(fetched[:, t, :], looked_up, ACT.Copy)
+            z_bf = keep.tile([P, HALF, PACK], BF16, name="z_bf%d" % half, tag="z_bf", align_bytes=64)
+            nc.vector.tensor_tensor(
+                z_bf[:].rearrange("p (c i) t -> p c t i", i=2),
+                gated[:, :, cols].rearrange("p t (c i) -> p c t i", i=2),
+                fetched[:].rearrange("p t (c i) -> p c t i", i=2),
+                ALU.add,
+            )
+            z_words = keep.tile([P, HALF], U32, name="z_words%d" % half, align_bytes=64)
+            z_scales = keep.tile([P, HALF], U8, name="z_scales%d" % half, align_bytes=64)
+            nc.vector.quantize_mx(z_words[:].bitcast(FP8X4), z_scales[:], z_bf[:].rearrange("p c t -> p (c t)"))
+            for t in range(PACK):
+                w_cols = slice(t * P, (t + 1) * P)
+                if t % 2 == 0:
+                    h_banks[half, t // 2] = psum.tile(
+                        [P, 2, HALF], F32, name="h_bank%d_%d" % (half, t // 2), tag="b_bank%d" % (2 * half + t // 2)
+                    )
+                nc.tensor.matmul_mx(
+                    h_banks[half, t // 2][:, t % 2, :],
+                    lhsT=w1_dealt[:, w_cols].bitcast(FP8X4), lhsT_scale=w1_dealt_scales[:, w_cols],
+                    rhs=z_words[:].bitcast(FP8X4), rhs_scale=z_scales[:],
+                    start=True, stop=True,
+                )
+            for t in range(PACK):
+                copy = nc.scalar.copy if half == 0 or t < 2 else nc.vector.tensor_copy
+                copy(h_rows[t][:, cols], h_banks[half, t // 2][:, t % 2, :])
+
+        out_rows = out_0.rearrange("(p t) j -> p t j", t=PACK)
+        out_words = words_of(out_1)
+        y_scales = keep.tile([P, S], U8, name="y_scales", align_bytes=64)
+        j0 = 0
+        for c, width in enumerate(CHUNKS):
+            cols = slice(j0, j0 + width)
+            entries = n3_list[:, j0 * MEMBERS // 16 : (j0 + width) * MEMBERS // 16]
+            y = keep.tile([P, PACK, width], F32, name="y%d" % c)
+            members = ring.tile([P, PACK, width * MEMBERS], F32, name="members", bufs=2)
+            for t in range(PACK):
+                if c == 0 and t >= 2:
+                    nc.vector.tensor_copy(members[:, t, :], h_rows[t][:].indirect(entries))
+                else:
+                    nc.scalar.activation(members[:, t, :], h_rows[t][:].indirect(entries), ACT.Copy)
+            four = members[:].rearrange("p t (j m) -> p (t j) m", m=MEMBERS)
+            high = ring.tile([P, PACK * width, 2], F32, name="high", bufs=2)
+            low = ring.tile([P, PACK * width, 2], F32, name="low", bufs=2)
+            nc.vector.tensor_tensor(high[:], four[:, :, 0:2], four[:, :, 2:4], ALU.max)
+            nc.vector.tensor_tensor(low[:], four[:, :, 0:2], four[:, :, 2:4], ALU.min)
+            largest = ring.tile([P, PACK, width], F32, name="largest", bufs=2)
+            smallest = ring.tile([P, PACK * width], F32, name="smallest", bufs=2)
+            nc.vector.tensor_tensor(largest[:].rearrange("p t j -> p (t j)"), high[:, :, 0], high[:, :, 1], ALU.max)
+            nc.vector.tensor_tensor(smallest[:], low[:, :, 0], low[:, :, 1], ALU.min)
+            capped = ring.tile([P, PACK, width], F32, name="capped", bufs=2)
+            for half in range(2):
+                first, last = max(j0, half * HALF), min(j0 + width, (half + 1) * HALF)
+                for pair in range(2 if first < last else 0):
+                    part = (slice(None), slice(2 * pair, 2 * pair + 2), slice(first - j0, last - j0))
+                    nc.vector.scalar_tensor_tensor(
+                        capped[part], h_banks[half, pair][:, :, first - half * HALF : last - half * HALF], 1.5,
+                        largest[part], ALU.mult, ALU.min,
+                    )
+            nc.vector.tensor_tensor(
+                y[:].rearrange("p t j -> p (t j)"), capped[:].rearrange("p t j -> p (t j)"), smallest[:], ALU.max
+            )
+            nc.sync.dma_start(out_rows[:, :, cols], y[:])
+            y_bf = keep.tile([P, width, PACK], BF16, name="y_bf%d" % c, align_bytes=64)
+            nc.vector.tensor_copy(y_bf[:].rearrange("p (c i) t -> p c t i", i=2), y[:].rearrange("p t (c i) -> p c t i", i=2))
+            y_words = keep.tile([P, width], U32, name="y_words%d" % c, align_bytes=64)
+            nc.vector.quantize_mx(y_words[:].bitcast(FP8X4), y_scales[:, cols], y_bf[:].rearrange("p c t -> p (c t)"))
+            nc.sync.dma_start(out_words[:, cols], y_words[:].bitcast(I32))
+            j0 += width
+        for q in range(4):
+            queue = nc.sync if q % 2 == 0 else nc.scalar
+            queue.dma_start(
+                out_2[0, 4 * q : 4 * q + 4, :].bitcast(I32), y_scales[32 * q : 32 * q + 4, :].bitcast(I32)
+            )

@@ -37,6 +37,7 @@ def tile_picked_twpqgatebgclip_none_po_kernel(
         lists = ctx.enter_context(tc.tile_pool(name="lists", bufs=1))
         keep = ctx.enter_context(tc.tile_pool(name="keep", bufs=1))
         ring = ctx.enter_context(tc.tile_pool(name="ring", bufs=3))
+        shared = ctx.enter_context(tc.tile_pool(name="shared", bufs=1))
         psum = ctx.enter_context(tc.psum_pool(name="psum", bufs=1))
 
         def load_list(dram, name):
@@ -83,8 +84,7 @@ def tile_picked_twpqgatebgclip_none_po_kernel(
                 plain.rearrange("p (c i t) -> p c t i", t=PACK, i=run),
             )
 
-        def coded_product(name, code_list, token_list, picked_tag, dealt_tag):
-            picked_scales = keep.tile([P, 2 * S], U8, name=name + "_picked_scales", tag="picked_scales")
+        def coded_product(name, code_list, token_list, picked_scales, x_picked, picked_tag, dealt_tag):
             placed_scales = keep.tile([P, 2 * S], U8, name=name + "_placed_scales", align_bytes=64)
             nc.vector.memset(placed_scales[:].bitcast(I32), 0)
             nc.vector.tensor_copy(picked_scales[:, S:], x_scale_table[:].indirect(token_list[:]))
@@ -93,7 +93,6 @@ def tile_picked_twpqgatebgclip_none_po_kernel(
                 nc.sync.dma_start(
                     placed_scales[r:P:32, :].bitcast(I32), picked_scales[8 * r : P : 32, :].bitcast(I32)
                 )
-            x_picked = keep.tile([P, S], U32, name=name + "_x_picked", tag="x_picked", align_bytes=64)
             nc.vector.tensor_copy(x_picked[:], x_word_table[:].indirect(token_list[:]))
             d_picked = keep.tile([P, S], U32, name=name + "_d_picked", tag=picked_tag, align_bytes=64)
             nc.vector.tensor_copy(d_picked[:], d_word_table[:].indirect(code_list[:]))
@@ -114,7 +113,12 @@ def tile_picked_twpqgatebgclip_none_po_kernel(
                 banks.append(bank)
             return banks
 
-        b_banks = coded_product("b", k2_list, two_list, "first_words", "second_words")
+        b_banks = coded_product(
+            "b", k2_list, two_list,
+            shared.tile([P, 2 * S], U8, name="b_picked_scales", offset=3 * S, align_bytes=64),
+            keep.tile([P, S], U32, name="b_x_picked", align_bytes=64),
+            "first_words", "second_words",
+        )
         n2_list = load_list(n2, "n2_list")
         gain = keep.tile([P, PACK], F32, name="gain")
         nc.sync.dma_start(gain[:], gn.rearrange("(p t) o -> p (t o)", t=PACK))
@@ -131,10 +135,15 @@ def tile_picked_twpqgatebgclip_none_po_kernel(
             nc.scalar.activation(gate_rows[t][:, :S], b_banks[t][:], ACT.Sigmoid, scale=0.0625)
             nc.scalar.activation(gate[:, t, :], gate_rows[t][:].indirect(n2_list[:]), ACT.Copy)
 
-        a_banks = coded_product("a", k1_list, offs_list, "second_words", "first_words")
+        a_banks = coded_product(
+            "a", k1_list, offs_list,
+            shared.tile([P, 2 * S], U8, name="a_picked_scales", offset=4 * S, align_bytes=64),
+            shared.tile([P, S], U32, name="a_x_picked", offset=0, align_bytes=64),
+            "second_words", "first_words",
+        )
 
         gain_a = keep.tile([P, PACK], F32, name="gain_a")
-        gain_half = keep.tile([P, PACK], F32, name="gain_half")
+        gain_half = keep.tile([P, PACK], F32, name="gain_half", tag="fetched1")
         nc.vector.tensor_scalar(gain_a[:], gain[:], 0.0625, None, ALU.mult)
         nc.vector.tensor_scalar(gain_half[:], gain[:], -0.03125, None, ALU.mult)
 
@@ -150,13 +159,10 @@ def tile_picked_twpqgatebgclip_none_po_kernel(
         h_banks = {}
         for half in range(2):
             cols = slice(half * HALF, (half + 1) * HALF)
-            fetched = keep.tile([P, PACK, HALF], F32, name="fetched%d" % half)
+            fetched = keep.tile([P, PACK, HALF], F32, name="fetched%d" % half, tag="fetched%d" % half)
             for t in range(PACK):
                 looked_up = half_rows[t][:].indirect(n1_list[:, half * HALF // 16 : (half + 1) * HALF // 16])
-                if half == 1 and t == PACK - 1:
-                    nc.vector.tensor_copy(fetched[:, t, :], looked_up)
-                else:
-                    nc.scalar.activation(fetched[:, t, :], looked_up, ACT.Copy)
+                nc.scalar.activation(fetched[:, t, :], looked_up, ACT.Copy)
             z_bf = keep.tile([P, HALF, PACK], BF16, name="z_bf%d" % half, tag="z_bf", align_bytes=64)
             nc.vector.tensor_tensor(
                 z_bf[:].rearrange("p (c i) t -> p c t i", i=2),
@@ -186,45 +192,55 @@ def tile_picked_twpqgatebgclip_none_po_kernel(
         out_rows = out_0.rearrange("(p t) j -> p t j", t=PACK)
         out_words = words_of(out_1)
         y_scales = keep.tile([P, S], U8, name="y_scales", align_bytes=64)
-        j0 = 0
-        for c, width in enumerate(CHUNKS):
-            cols = slice(j0, j0 + width)
+        starts = [sum(CHUNKS[:c]) for c in range(len(CHUNKS))]
+        y_chunks = []
+        for c, (j0, width) in enumerate(zip(starts, CHUNKS)):
             entries = n3_list[:, j0 * MEMBERS // 16 : (j0 + width) * MEMBERS // 16]
             y = keep.tile([P, PACK, width], F32, name="y%d" % c)
-            members = ring.tile([P, PACK, width * MEMBERS], F32, name="members", bufs=2)
-            for t in range(PACK):
-                if c == 0 and t >= 2:
-                    nc.vector.tensor_copy(members[:, t, :], h_rows[t][:].indirect(entries))
-                else:
-                    nc.scalar.activation(members[:, t, :], h_rows[t][:].indirect(entries), ACT.Copy)
-            four = members[:].rearrange("p t (j m) -> p (t j) m", m=MEMBERS)
-            high = ring.tile([P, PACK * width, 2], F32, name="high", bufs=2)
-            low = ring.tile([P, PACK * width, 2], F32, name="low", bufs=2)
-            nc.vector.tensor_tensor(high[:], four[:, :, 0:2], four[:, :, 2:4], ALU.max)
-            nc.vector.tensor_tensor(low[:], four[:, :, 0:2], four[:, :, 2:4], ALU.min)
-            largest = ring.tile([P, PACK, width], F32, name="largest", bufs=2)
-            smallest = ring.tile([P, PACK * width], F32, name="smallest", bufs=2)
-            nc.vector.tensor_tensor(largest[:].rearrange("p t j -> p (t j)"), high[:, :, 0], high[:, :, 1], ALU.max)
-            nc.vector.tensor_tensor(smallest[:], low[:, :, 0], low[:, :, 1], ALU.min)
-            capped = ring.tile([P, PACK, width], F32, name="capped", bufs=2)
-            for half in range(2):
-                first, last = max(j0, half * HALF), min(j0 + width, (half + 1) * HALF)
-                for pair in range(2 if first < last else 0):
-                    part = (slice(None), slice(2 * pair, 2 * pair + 2), slice(first - j0, last - j0))
+            for pair in range(2):
+                members = keep.tile([P, 2, width * MEMBERS], F32, name="members%d_%d" % (c, pair))
+                for u in range(2):
+                    looked_up = h_rows[2 * pair + u][:].indirect(entries)
+                    if c == 0 and pair == 1:
+                        nc.vector.tensor_copy(members[:, u, :], looked_up)
+                    else:
+                        nc.scalar.activation(members[:, u, :], looked_up, ACT.Copy)
+                four = members[:].rearrange("p u (j m) -> p (u j) m", m=MEMBERS)
+                high = ring.tile([P, 2 * width, 2], F32, name="high")
+                low = ring.tile([P, 2 * width, 2], F32, name="low")
+                nc.vector.tensor_tensor(high[:], four[:, :, 0:2], four[:, :, 2:4], ALU.max)
+                nc.vector.tensor_tensor(low[:], four[:, :, 0:2], four[:, :, 2:4], ALU.min)
+                largest = ring.tile([P, 2, width], F32, name="largest")
+                smallest = ring.tile([P, 2 * width], F32, name="smallest")
+                nc.vector.tensor_tensor(largest[:].rearrange("p u j -> p (u j)"), high[:, :, 0], high[:, :, 1], ALU.max)
+                nc.vector.tensor_tensor(smallest[:], low[:, :, 0], low[:, :, 1], ALU.min)
+                capped = ring.tile([P, 2, width], F32, name="capped")
+                for half in range(j0 // HALF, (j0 + width - 1) // HALF + 1):
+                    first, last = max(j0, half * HALF), min(j0 + width, (half + 1) * HALF)
                     nc.vector.scalar_tensor_tensor(
-                        capped[part], h_banks[half, pair][:, :, first - half * HALF : last - half * HALF], 1.5,
-                        largest[part], ALU.mult, ALU.min,
+                        capped[:, :, first - j0 : last - j0],
+                        h_banks[half, pair][:, :, first - half * HALF : last - half * HALF],
+                        1.5,
+                        largest[:, :, first - j0 : last - j0],
+                        ALU.mult,
+                        ALU.min,
                     )
-            nc.vector.tensor_tensor(
-                y[:].rearrange("p t j -> p (t j)"), capped[:].rearrange("p t j -> p (t j)"), smallest[:], ALU.max
-            )
-            nc.sync.dma_start(out_rows[:, :, cols], y[:])
+                nc.vector.tensor_tensor(
+                    y[:, 2 * pair : 2 * pair + 2, :].rearrange("p u j -> p (u j)"),
+                    capped[:].rearrange("p u j -> p (u j)"),
+                    smallest[:],
+                    ALU.max,
+                )
+            nc.sync.dma_start(out_rows[:, :, j0 : j0 + width], y[:])
+            y_chunks.append(y)
+        for c, (j0, width) in enumerate(zip(starts, CHUNKS)):
+            cols = slice(j0, j0 + width)
             y_bf = keep.tile([P, width, PACK], BF16, name="y_bf%d" % c, align_bytes=64)
-            nc.vector.tensor_copy(y_bf[:].rearrange("p (c i) t -> p c t i", i=2), y[:].rearrange("p t (c i) -> p c t i", i=2))
+            cast = nc.vector.tensor_copy if c == len(CHUNKS) - 1 else nc.scalar.copy
+            cast(y_bf[:].rearrange("p (c i) t -> p c t i", i=2), y_chunks[c][:].rearrange("p t (c i) -> p c t i", i=2))
             y_words = keep.tile([P, width], U32, name="y_words%d" % c, align_bytes=64)
             nc.vector.quantize_mx(y_words[:].bitcast(FP8X4), y_scales[:, cols], y_bf[:].rearrange("p c t -> p (c t)"))
             nc.sync.dma_start(out_words[:, cols], y_words[:].bitcast(I32))
-            j0 += width
         for q in range(4):
             queue = nc.sync if q % 2 == 0 else nc.scalar
             queue.dma_start(

@@ -20,7 +20,7 @@ CODEWORDS = 2048
 MEMBERS = 4
 SPARE = 32
 HALF = S // 2
-CHUNKS = (64, 128, 128, 128, 64)
+CHUNKS = (128, 128, 128, 128)
 FLOPS = 3 * 2 * 512 * 512 * 512
 
 
@@ -48,7 +48,7 @@ def tile_picked_twpqgatebgclip_none_po_kernel(
         d_scale_table = keep.tile([P, CODEWORDS], U8, name="d_scale_table")
         x_scale_table = keep.tile([P, TOKENS], U8, name="x_scale_table")
         nc.gpsimd.memset(x_scale_table[:].bitcast(I32), 0)
-        nc.gpsimd.memset(d_scale_table[:].bitcast(I32), 0)
+        nc.vector.memset(d_scale_table[:].bitcast(I32), 0)
 
         two_list = load_list(two, "two_list")
         k2_list = load_list(k2, "k2_list")
@@ -60,15 +60,6 @@ def tile_picked_twpqgatebgclip_none_po_kernel(
         nc.sync.dma_start(d_word_table[:].bitcast(I32), words_of(d_words))
         k1_list = load_list(k1, "k1_list")
         offs_list = load_list(offs, "offs_list")
-
-        w1_scale_rows = keep.tile([P, S], U8, name="w1_scale_rows")
-        nc.vector.memset(w1_scale_rows[:].bitcast(I32), 0)
-        for q in range(4):
-            nc.gpsimd.dma_start(
-                w1_scale_rows[32 * q : 32 * q + 4, :].bitcast(I32), w1_scales[0, 4 * q : 4 * q + 4, :].bitcast(I32)
-            )
-        w1_word_rows = keep.tile([P, S], U32, name="w1_word_rows")
-        nc.gpsimd.dma_start(w1_word_rows[:].bitcast(I32), words_of(w1_words))
 
         def window(name):
             tile = keep.tile([P, S + SPARE], F32, name=name)
@@ -124,11 +115,15 @@ def tile_picked_twpqgatebgclip_none_po_kernel(
         nc.sync.dma_start(gain[:], gn.rearrange("(p t) o -> p (t o)", t=PACK))
         n1_list = load_list(n1, "n1_list")
         n3_list = load_list(n3, "n3_list")
+        w1_scale_rows = keep.tile([P, S], U8, name="w1_scale_rows")
+        nc.vector.memset(w1_scale_rows[:].bitcast(I32), 0)
+        for q in range(4):
+            nc.sync.dma_start(
+                w1_scale_rows[32 * q : 32 * q + 4, :].bitcast(I32), w1_scales[0, 4 * q : 4 * q + 4, :].bitcast(I32)
+            )
+        w1_word_rows = keep.tile([P, S], U32, name="w1_word_rows")
+        nc.sync.dma_start(w1_word_rows[:].bitcast(I32), words_of(w1_words))
 
-        w1_dealt = keep.tile([P, S], U32, name="w1_dealt", align_bytes=64)
-        deal(nc.gpsimd.tensor_copy, w1_dealt[:], w1_word_rows[:], 4)
-        w1_dealt_scales = keep.tile([P, S], U8, name="w1_dealt_scales", align_bytes=64)
-        deal(nc.gpsimd.tensor_copy, w1_dealt_scales[:], w1_scale_rows[:], 16)
 
         gate = keep.tile([P, PACK, S], F32, name="gate")
         for t in range(PACK):
@@ -142,6 +137,11 @@ def tile_picked_twpqgatebgclip_none_po_kernel(
             "second_words", "first_words",
         )
 
+        w1_dealt_scales = shared.tile([P, S], U8, name="w1_dealt_scales", offset=4 * S, align_bytes=64)
+        deal(nc.vector.tensor_copy, w1_dealt_scales[:], w1_scale_rows[:], 16)
+        w1_dealt = shared.tile([P, S], U32, name="w1_dealt", offset=5 * S, align_bytes=64)
+        deal(nc.vector.tensor_copy, w1_dealt[:], w1_word_rows[:], 4)
+
         gain_a = keep.tile([P, PACK], F32, name="gain_a")
         gain_half = keep.tile([P, PACK], F32, name="gain_half", tag="fetched1")
         nc.vector.tensor_scalar(gain_a[:], gain[:], 0.0625, None, ALU.mult)
@@ -150,23 +150,23 @@ def tile_picked_twpqgatebgclip_none_po_kernel(
         half_rows = [keep.tile([P, S], F32, name="half_rows%d" % t) for t in range(PACK)]
         for t in range(PACK):
             nc.vector.tensor_scalar(half_rows[t][:], a_banks[t][:], gain_half[:, t : t + 1], None, ALU.mult)
-        gated = keep.tile([P, PACK, S], F32, name="gated")
-        for t in range(PACK):
-            nc.vector.scalar_tensor_tensor(
-                gated[:, t, :], a_banks[t][:], gain_a[:, t : t + 1], gate[:, t, :], ALU.mult, ALU.mult
-            )
 
         h_banks = {}
         for half in range(2):
             cols = slice(half * HALF, (half + 1) * HALF)
+            gated = keep.tile([P, PACK, HALF], F32, name="gated%d" % half)
+            for t in range(PACK):
+                nc.vector.scalar_tensor_tensor(
+                    gated[:, t, :], a_banks[t][:, cols], gain_a[:, t : t + 1], gate[:, t, cols], ALU.mult, ALU.mult
+                )
             fetched = keep.tile([P, PACK, HALF], F32, name="fetched%d" % half, tag="fetched%d" % half)
             for t in range(PACK):
                 looked_up = half_rows[t][:].indirect(n1_list[:, half * HALF // 16 : (half + 1) * HALF // 16])
                 nc.scalar.activation(fetched[:, t, :], looked_up, ACT.Copy)
-            z_bf = keep.tile([P, HALF, PACK], BF16, name="z_bf%d" % half, tag="z_bf", align_bytes=64)
+            z_bf = keep.tile([P, HALF, PACK], BF16, name="z_bf%d" % half, align_bytes=64)
             nc.vector.tensor_tensor(
                 z_bf[:].rearrange("p (c i) t -> p c t i", i=2),
-                gated[:, :, cols].rearrange("p t (c i) -> p c t i", i=2),
+                gated[:].rearrange("p t (c i) -> p c t i", i=2),
                 fetched[:].rearrange("p t (c i) -> p c t i", i=2),
                 ALU.add,
             )
@@ -193,46 +193,70 @@ def tile_picked_twpqgatebgclip_none_po_kernel(
         out_words = words_of(out_1)
         y_scales = keep.tile([P, S], U8, name="y_scales", align_bytes=64)
         starts = [sum(CHUNKS[:c]) for c in range(len(CHUNKS))]
-        y_chunks = []
-        for c, (j0, width) in enumerate(zip(starts, CHUNKS)):
+        y_chunks = [keep.tile([P, PACK, width], F32, name="y%d" % c) for c, width in enumerate(CHUNKS)]
+        units = [(c, pair) for c in range(len(CHUNKS)) for pair in range(2)]
+        largest, smallest, capped = {}, {}, {}
+
+        def fetch(c, pair):
+            j0, width = starts[c], CHUNKS[c]
             entries = n3_list[:, j0 * MEMBERS // 16 : (j0 + width) * MEMBERS // 16]
-            y = keep.tile([P, PACK, width], F32, name="y%d" % c)
-            for pair in range(2):
-                members = keep.tile([P, 2, width * MEMBERS], F32, name="members%d_%d" % (c, pair))
-                for u in range(2):
-                    looked_up = h_rows[2 * pair + u][:].indirect(entries)
-                    if c == 0 and pair == 1:
-                        nc.vector.tensor_copy(members[:, u, :], looked_up)
-                    else:
-                        nc.scalar.activation(members[:, u, :], looked_up, ACT.Copy)
-                four = members[:].rearrange("p u (j m) -> p (u j) m", m=MEMBERS)
-                high = ring.tile([P, 2 * width, 2], F32, name="high")
-                low = ring.tile([P, 2 * width, 2], F32, name="low")
-                nc.vector.tensor_tensor(high[:], four[:, :, 0:2], four[:, :, 2:4], ALU.max)
-                nc.vector.tensor_tensor(low[:], four[:, :, 0:2], four[:, :, 2:4], ALU.min)
-                largest = ring.tile([P, 2, width], F32, name="largest")
-                smallest = ring.tile([P, 2 * width], F32, name="smallest")
-                nc.vector.tensor_tensor(largest[:].rearrange("p u j -> p (u j)"), high[:, :, 0], high[:, :, 1], ALU.max)
-                nc.vector.tensor_tensor(smallest[:], low[:, :, 0], low[:, :, 1], ALU.min)
-                capped = ring.tile([P, 2, width], F32, name="capped")
-                for half in range(j0 // HALF, (j0 + width - 1) // HALF + 1):
-                    first, last = max(j0, half * HALF), min(j0 + width, (half + 1) * HALF)
-                    nc.vector.scalar_tensor_tensor(
-                        capped[:, :, first - j0 : last - j0],
-                        h_banks[half, pair][:, :, first - half * HALF : last - half * HALF],
-                        1.5,
-                        largest[:, :, first - j0 : last - j0],
-                        ALU.mult,
-                        ALU.min,
-                    )
-                nc.vector.tensor_tensor(
-                    y[:, 2 * pair : 2 * pair + 2, :].rearrange("p u j -> p (u j)"),
-                    capped[:].rearrange("p u j -> p (u j)"),
-                    smallest[:],
-                    ALU.max,
+            members = keep.tile([P, 2, width * MEMBERS], F32, name="members%d_%d" % (c, pair))
+            for u in range(2):
+                looked_up = h_rows[2 * pair + u][:].indirect(entries)
+                if c == 0 and 2 * pair + u == 1:
+                    nc.vector.tensor_copy(members[:, u, :], looked_up)
+                else:
+                    nc.scalar.activation(members[:, u, :], looked_up, ACT.Copy)
+            return members[:].rearrange("p u (j m) -> p (u j) m", m=MEMBERS)
+
+        def halve(four, op, name):
+            two_left = ring.tile([P, four.shape[1], 2], F32, name=name)
+            nc.vector.tensor_tensor(two_left[:], four[:, :, 0:2], four[:, :, 2:4], op)
+            return two_left
+
+        def finish(two_left, op, name):
+            one_left = ring.tile([P, two_left.shape[1]], F32, name=name)
+            nc.vector.tensor_tensor(one_left[:], two_left[:, :, 0], two_left[:, :, 1], op)
+            return one_left
+
+        def cap(c, pair):
+            j0, width = starts[c], CHUNKS[c]
+            capped[c, pair] = ring.tile([P, 2, width], F32, name="capped")
+            top = largest[c, pair][:].rearrange("p (u j) -> p u j", u=2)
+            for half in range(j0 // HALF, (j0 + width - 1) // HALF + 1):
+                first, last = max(j0, half * HALF), min(j0 + width, (half + 1) * HALF)
+                nc.vector.scalar_tensor_tensor(
+                    capped[c, pair][:, :, first - j0 : last - j0],
+                    h_banks[half, pair][:, :, first - half * HALF : last - half * HALF],
+                    1.5,
+                    top[:, :, first - j0 : last - j0],
+                    ALU.mult,
+                    ALU.min,
                 )
-            nc.sync.dma_start(out_rows[:, :, j0 : j0 + width], y[:])
-            y_chunks.append(y)
+
+        def floor(c, pair):
+            nc.vector.tensor_tensor(
+                y_chunks[c][:, 2 * pair : 2 * pair + 2, :].rearrange("p u j -> p (u j)"),
+                capped[c, pair][:].rearrange("p u j -> p (u j)"),
+                smallest[c, pair][:],
+                ALU.max,
+            )
+            if pair == 1:
+                nc.sync.dma_start(out_rows[:, :, starts[c] : starts[c] + CHUNKS[c]], y_chunks[c][:])
+
+        for before, unit in zip([None] + units, units):
+            four = fetch(*unit)
+            high = halve(four, ALU.max, "high")
+            if before:
+                cap(*before)
+            low = halve(four, ALU.min, "low")
+            if before:
+                floor(*before)
+            largest[unit] = finish(high, ALU.max, "largest")
+            smallest[unit] = finish(low, ALU.min, "smallest")
+        cap(*units[-1])
+        floor(*units[-1])
+
         for c, (j0, width) in enumerate(zip(starts, CHUNKS)):
             cols = slice(j0, j0 + width)
             y_bf = keep.tile([P, width, PACK], BF16, name="y_bf%d" % c, align_bytes=64)

@@ -21,6 +21,7 @@ MEMBERS = 4
 SPARE = 32
 HALF = S // 2
 CHUNKS = (128, 128, 128, 128)
+VECTOR_ENTRIES = (512, 256)
 FLOPS = 3 * 2 * 512 * 512 * 512
 
 
@@ -199,30 +200,37 @@ def tile_picked_twpqgatebgclip_none_po_kernel(
 
         def fetch(c, pair):
             j0, width = starts[c], CHUNKS[c]
-            entries = n3_list[:, j0 * MEMBERS // 16 : (j0 + width) * MEMBERS // 16]
-            members = keep.tile([P, 2, width * MEMBERS], F32, name="members%d_%d" % (c, pair))
+            count = width * MEMBERS
+            members = keep.tile([P, 2, count], F32, name="members%d_%d" % (c, pair))
             for u in range(2):
-                looked_up = h_rows[2 * pair + u][:].indirect(entries)
-                if c == 0 and 2 * pair + u == 1:
-                    nc.vector.tensor_copy(members[:, u, :], looked_up)
-                else:
-                    nc.scalar.activation(members[:, u, :], looked_up, ACT.Copy)
-            return members[:].rearrange("p u (j m) -> p (u j) m", m=MEMBERS)
+                on_vector = VECTOR_ENTRIES[pair] if c == 0 and u == 1 else 0
+                split = count - on_vector
+                first = j0 * MEMBERS // 16
+                rows = h_rows[2 * pair + u]
+                if split > 0:
+                    entries = n3_list[:, first : first + split // 16]
+                    nc.scalar.activation(members[:, u, :split], rows[:].indirect(entries), ACT.Copy)
+                if on_vector > 0:
+                    entries = n3_list[:, first + split // 16 : first + count // 16]
+                    nc.vector.tensor_copy(members[:, u, split:], rows[:].indirect(entries))
+            return members[:].rearrange("p u (a i m) -> p (u a) i m", i=2, m=MEMBERS)
 
         def halve(four, op, name):
-            two_left = ring.tile([P, four.shape[1], 2], F32, name=name)
-            nc.vector.tensor_tensor(two_left[:], four[:, :, 0:2], four[:, :, 2:4], op)
+            two_left = ring.tile([P, four.shape[1], 2, 2], F32, name=name)
+            nc.vector.tensor_tensor(
+                two_left[:].rearrange("p a m i -> p a i m"), four[:, :, :, 0:2], four[:, :, :, 2:4], op
+            )
             return two_left
 
         def finish(two_left, op, name):
-            one_left = ring.tile([P, two_left.shape[1]], F32, name=name)
-            nc.vector.tensor_tensor(one_left[:], two_left[:, :, 0], two_left[:, :, 1], op)
+            one_left = ring.tile([P, two_left.shape[1], 2], F32, name=name)
+            nc.vector.tensor_tensor(one_left[:], two_left[:, :, 0, :], two_left[:, :, 1, :], op)
             return one_left
 
         def cap(c, pair):
             j0, width = starts[c], CHUNKS[c]
             capped[c, pair] = ring.tile([P, 2, width], F32, name="capped")
-            top = largest[c, pair][:].rearrange("p (u j) -> p u j", u=2)
+            top = largest[c, pair][:].rearrange("p (u a) i -> p u (a i)", u=2)
             for half in range(j0 // HALF, (j0 + width - 1) // HALF + 1):
                 first, last = max(j0, half * HALF), min(j0 + width, (half + 1) * HALF)
                 nc.vector.scalar_tensor_tensor(
@@ -238,7 +246,7 @@ def tile_picked_twpqgatebgclip_none_po_kernel(
             nc.vector.tensor_tensor(
                 y_chunks[c][:, 2 * pair : 2 * pair + 2, :].rearrange("p u j -> p (u j)"),
                 capped[c, pair][:].rearrange("p u j -> p (u j)"),
-                smallest[c, pair][:],
+                smallest[c, pair][:].rearrange("p a i -> p (a i)"),
                 ALU.max,
             )
             if pair == 1:

from contextlib import ExitStack

import concourse.mybir as mybir

F32 = mybir.dt.float32
BF16 = mybir.dt.bfloat16
I32 = mybir.dt.int32
U32 = mybir.dt.uint32
U16 = mybir.dt.uint16
U8 = mybir.dt.uint8
FP8X4 = mybir.dt.float8_e4m3fn_x4
ALU = mybir.AluOpType
ACT = mybir.ActivationFunctionType

P = 128
PACK = 4
S = 512
TOKENS = 1024
CODEWORDS = 2048
MEMBERS = 4
SPARE = 32
HALF = S // 2
CHUNKS = (128, 128, 128, 128)
VECTOR_ENTRIES = (512, 256)
FLOPS = 3 * 2 * 512 * 512 * 512


def tile_picked_twpqgatebgclip_none_po_kernel(
    tc, x_words, x_scales, d_words, d_scales, gn, w1_words, w1_scales,
    offs, k1, two, k2, n1, n2, n3, out_0, out_1, out_2,
):
    nc = tc.nc

    def words_of(dram):
        return dram[0].rearrange("p n t -> p (n t)").bitcast(I32)

    with ExitStack() as ctx:
        lists = ctx.enter_context(tc.tile_pool(name="lists", bufs=1))
        keep = ctx.enter_context(tc.tile_pool(name="keep", bufs=1))
        ring = ctx.enter_context(tc.tile_pool(name="ring", bufs=3))
        shared = ctx.enter_context(tc.tile_pool(name="shared", bufs=1))
        psum = ctx.enter_context(tc.psum_pool(name="psum", bufs=1))

        def load_list(dram, name):
            tile = lists.tile([P, dram.shape[1]], U16, name=name)
            nc.sync.dma_start(tile[:], dram)
            return tile

        d_scale_table = keep.tile([P, CODEWORDS], U8, name="d_scale_table")
        x_scale_table = keep.tile([P, TOKENS], U8, name="x_scale_table")
        nc.gpsimd.memset(x_scale_table[:].bitcast(I32), 0)
        nc.vector.memset(d_scale_table[:].bitcast(I32), 0)

        two_list = load_list(two, "two_list")
        k2_list = load_list(k2, "k2_list")
        nc.sync.dma_start(x_scale_table[0:P:8, :].bitcast(I32), x_scales[0].bitcast(I32))
        nc.sync.dma_start(d_scale_table[0:P:8, :].bitcast(I32), d_scales[0].bitcast(I32))
        x_word_table = keep.tile([P, TOKENS], U32, name="x_word_table")
        nc.sync.dma_start(x_word_table[:].bitcast(I32), words_of(x_words))
        d_word_table = keep.tile([P, CODEWORDS], U32, name="d_word_table")
        nc.sync.dma_start(d_word_table[:].bitcast(I32), words_of(d_words))
        k1_list = load_list(k1, "k1_list")
        offs_list = load_list(offs, "offs_list")

        def window(name):
            tile = keep.tile([P, S + SPARE], F32, name=name)
            nc.vector.memset(tile[:, S:], 0.0)
            return tile

        gate_rows = [window("gate_rows%d" % t) for t in range(PACK)]
        h_rows = [window("h_rows%d" % t) for t in range(PACK)]

        def deal(copy, dealt, plain, run):
            copy(
                dealt.rearrange("p (t c i) -> p c t i", t=PACK, i=run),
                plain.rearrange("p (c i t) -> p c t i", t=PACK, i=run),
            )

        def coded_product(name, code_list, token_list, picked_scales, x_picked, picked_tag, dealt_tag):
            placed_scales = keep.tile([P, 2 * S], U8, name=name + "_placed_scales", align_bytes=64)
            nc.vector.memset(placed_scales[:].bitcast(I32), 0)
            nc.vector.tensor_copy(picked_scales[:, S:], x_scale_table[:].indirect(token_list[:]))
            nc.vector.tensor_copy(picked_scales[:, :S], d_scale_table[:].indirect(code_list[:]))
            for r in range(4):
                nc.sync.dma_start(
                    placed_scales[r:P:32, :].bitcast(I32), picked_scales[8 * r : P : 32, :].bitcast(I32)
                )
            nc.vector.tensor_copy(x_picked[:], x_word_table[:].indirect(token_list[:]))
            d_picked = keep.tile([P, S], U32, name=name + "_d_picked", tag=picked_tag, align_bytes=64)
            nc.vector.tensor_copy(d_picked[:], d_word_table[:].indirect(code_list[:]))
            d_dealt = keep.tile([P, S], U32, name=name + "_d_dealt", tag=dealt_tag, align_bytes=64)
            deal(nc.vector.tensor_copy, d_dealt[:], d_picked[:], 4)
            d_dealt_scales = keep.tile([P, S], U8, name=name + "_d_dealt_scales", align_bytes=64)
            deal(nc.vector.tensor_copy, d_dealt_scales[:], placed_scales[:, :S], 16)
            banks = []
            for t in range(PACK):
                cols = slice(t * P, (t + 1) * P)
                bank = psum.tile([P, S], F32, name=name + "_bank%d" % t, tag=name + "_bank%d" % t)
                nc.tensor.matmul_mx(
                    bank[:],
                    lhsT=d_dealt[:, cols].bitcast(FP8X4), lhsT_scale=d_dealt_scales[:, cols],
                    rhs=x_picked[:].bitcast(FP8X4), rhs_scale=placed_scales[:, S:],
                    start=True, stop=True,
                )
                banks.append(bank)
            return banks

        b_banks = coded_product(
            "b", k2_list, two_list,
            shared.tile([P, 2 * S], U8, name="b_picked_scales", offset=3 * S, align_bytes=64),
            keep.tile([P, S], U32, name="b_x_picked", align_bytes=64),
            "first_words", "second_words",
        )
        n2_list = load_list(n2, "n2_list")
        gain = keep.tile([P, PACK], F32, name="gain")
        nc.sync.dma_start(gain[:], gn.rearrange("(p t) o -> p (t o)", t=PACK))
        n1_list = load_list(n1, "n1_list")
        n3_list = load_list(n3, "n3_list")
        w1_scale_rows = keep.tile([P, S], U8, name="w1_scale_rows")
        nc.vector.memset(w1_scale_rows[:].bitcast(I32), 0)
        for q in range(4):
            nc.sync.dma_start(
                w1_scale_rows[32 * q : 32 * q + 4, :].bitcast(I32), w1_scales[0, 4 * q : 4 * q + 4, :].bitcast(I32)
            )
        w1_word_rows = keep.tile([P, S], U32, name="w1_word_rows")
        nc.sync.dma_start(w1_word_rows[:].bitcast(I32), words_of(w1_words))


        gate = keep.tile([P, PACK, S], F32, name="gate")
        for t in range(PACK):
            nc.scalar.activation(gate_rows[t][:, :S], b_banks[t][:], ACT.Sigmoid, scale=0.0625)
            nc.scalar.activation(gate[:, t, :], gate_rows[t][:].indirect(n2_list[:]), ACT.Copy)

        a_banks = coded_product(
            "a", k1_list, offs_list,
            shared.tile([P, 2 * S], U8, name="a_picked_scales", offset=4 * S, align_bytes=64),
            shared.tile([P, S], U32, name="a_x_picked", offset=0, align_bytes=64),
            "second_words", "first_words",
        )

        w1_dealt_scales = shared.tile([P, S], U8, name="w1_dealt_scales", offset=4 * S, align_bytes=64)
        deal(nc.vector.tensor_copy, w1_dealt_scales[:], w1_scale_rows[:], 16)
        w1_dealt = shared.tile([P, S], U32, name="w1_dealt", offset=5 * S, align_bytes=64)
        deal(nc.vector.tensor_copy, w1_dealt[:], w1_word_rows[:], 4)

        gain_a = keep.tile([P, PACK], F32, name="gain_a")
        gain_half = keep.tile([P, PACK], F32, name="gain_half", tag="fetched1")
        nc.vector.tensor_scalar(gain_a[:], gain[:], 0.0625, None, ALU.mult)
        nc.vector.tensor_scalar(gain_half[:], gain[:], -0.03125, None, ALU.mult)

        half_rows = [keep.tile([P, S], F32, name="half_rows%d" % t) for t in range(PACK)]
        for t in range(PACK):
            nc.vector.tensor_scalar(half_rows[t][:], a_banks[t][:], gain_half[:, t : t + 1], None, ALU.mult)

        h_banks = {}
        for half in range(2):
            cols = slice(half * HALF, (half + 1) * HALF)
            gated = keep.tile([P, PACK, HALF], F32, name="gated%d" % half)
            for t in range(PACK):
                nc.vector.scalar_tensor_tensor(
                    gated[:, t, :], a_banks[t][:, cols], gain_a[:, t : t + 1], gate[:, t, cols], ALU.mult, ALU.mult
                )
            fetched = keep.tile([P, PACK, HALF], F32, name="fetched%d" % half, tag="fetched%d" % half)
            for t in range(PACK):
                looked_up = half_rows[t][:].indirect(n1_list[:, half * HALF // 16 : (half + 1) * HALF // 16])
                nc.scalar.activation(fetched[:, t, :], looked_up, ACT.Copy)
            z_bf = keep.tile([P, HALF, PACK], BF16, name="z_bf%d" % half, align_bytes=64)
            nc.vector.tensor_tensor(
                z_bf[:].rearrange("p (c i) t -> p c t i", i=2),
                gated[:].rearrange("p t (c i) -> p c t i", i=2),
                fetched[:].rearrange("p t (c i) -> p c t i", i=2),
                ALU.add,
            )
            z_words = keep.tile([P, HALF], U32, name="z_words%d" % half, align_bytes=64)
            z_scales = keep.tile([P, HALF], U8, name="z_scales%d" % half, align_bytes=64)
            nc.vector.quantize_mx(z_words[:].bitcast(FP8X4), z_scales[:], z_bf[:].rearrange("p c t -> p (c t)"))
            for t in range(PACK):
                w_cols = slice(t * P, (t + 1) * P)
                if t % 2 == 0:
                    h_banks[half, t // 2] = psum.tile(
                        [P, 2, HALF], F32, name="h_bank%d_%d" % (half, t // 2), tag="b_bank%d" % (2 * half + t // 2)
                    )
                nc.tensor.matmul_mx(
                    h_banks[half, t // 2][:, t % 2, :],
                    lhsT=w1_dealt[:, w_cols].bitcast(FP8X4), lhsT_scale=w1_dealt_scales[:, w_cols],
                    rhs=z_words[:].bitcast(FP8X4), rhs_scale=z_scales[:],
                    start=True, stop=True,
                )
            for t in range(PACK):
                copy = nc.scalar.copy if half == 0 or t < 2 else nc.vector.tensor_copy
                copy(h_rows[t][:, cols], h_banks[half, t // 2][:, t % 2, :])

        out_rows = out_0.rearrange("(p t) j -> p t j", t=PACK)
        out_words = words_of(out_1)
        y_scales = keep.tile([P, S], U8, name="y_scales", align_bytes=64)
        starts = [sum(CHUNKS[:c]) for c in range(len(CHUNKS))]
        y_chunks = [keep.tile([P, PACK, width], F32, name="y%d" % c) for c, width in enumerate(CHUNKS)]
        units = [(c, pair) for c in range(len(CHUNKS)) for pair in range(2)]
        largest, smallest, capped = {}, {}, {}

        def fetch(c, pair):
            j0, width = starts[c], CHUNKS[c]
            count = width * MEMBERS
            members = keep.tile([P, 2, count], F32, name="members%d_%d" % (c, pair))
            for u in range(2):
                on_vector = VECTOR_ENTRIES[pair] if c == 0 and u == 1 else 0
                split = count - on_vector
                first = j0 * MEMBERS // 16
                rows = h_rows[2 * pair + u]
                if split > 0:
                    entries = n3_list[:, first : first + split // 16]
                    nc.scalar.activation(members[:, u, :split], rows[:].indirect(entries), ACT.Copy)
                if on_vector > 0:
                    entries = n3_list[:, first + split // 16 : first + count // 16]
                    nc.vector.tensor_copy(members[:, u, split:], rows[:].indirect(entries))
            return members[:].rearrange("p u (a i m) -> p (u a) i m", i=2, m=MEMBERS)

        def halve(four, op, name):
            two_left = ring.tile([P, four.shape[1], 2, 2], F32, name=name)
            nc.vector.tensor_tensor(
                two_left[:].rearrange("p a m i -> p a i m"), four[:, :, :, 0:2], four[:, :, :, 2:4], op
            )
            return two_left

        def finish(two_left, op, name):
            one_left = ring.tile([P, two_left.shape[1], 2], F32, name=name)
            nc.vector.tensor_tensor(one_left[:], two_left[:, :, 0, :], two_left[:, :, 1, :], op)
            return one_left

        def cap(c, pair):
            j0, width = starts[c], CHUNKS[c]
            capped[c, pair] = ring.tile([P, 2, width], F32, name="capped")
            top = largest[c, pair][:].rearrange("p (u a) i -> p u (a i)", u=2)
            for half in range(j0 // HALF, (j0 + width - 1) // HALF + 1):
                first, last = max(j0, half * HALF), min(j0 + width, (half + 1) * HALF)
                nc.vector.scalar_tensor_tensor(
                    capped[c, pair][:, :, first - j0 : last - j0],
                    h_banks[half, pair][:, :, first - half * HALF : last - half * HALF],
                    1.5,
                    top[:, :, first - j0 : last - j0],
                    ALU.mult,
                    ALU.min,
                )

        def floor(c, pair):
            nc.vector.tensor_tensor(
                y_chunks[c][:, 2 * pair : 2 * pair + 2, :].rearrange("p u j -> p (u j)"),
                capped[c, pair][:].rearrange("p u j -> p (u j)"),
                smallest[c, pair][:].rearrange("p a i -> p (a i)"),
                ALU.max,
            )
            if pair == 1:
                nc.sync.dma_start(out_rows[:, :, starts[c] : starts[c] + CHUNKS[c]], y_chunks[c][:])

        for before, unit in zip([None] + units, units):
            four = fetch(*unit)
            high = halve(four, ALU.max, "high")
            if before:
                cap(*before)
            low = halve(four, ALU.min, "low")
            if before:
                floor(*before)
            largest[unit] = finish(high, ALU.max, "largest")
            smallest[unit] = finish(low, ALU.min, "smallest")
        cap(*units[-1])
        floor(*units[-1])

        for c, (j0, width) in enumerate(zip(starts, CHUNKS)):
            cols = slice(j0, j0 + width)
            y_bf = keep.tile([P, width, PACK], BF16, name="y_bf%d" % c, align_bytes=64)
            cast = nc.vector.tensor_copy if c == len(CHUNKS) - 1 else nc.scalar.copy
            cast(y_bf[:].rearrange("p (c i) t -> p c t i", i=2), y_chunks[c][:].rearrange("p t (c i) -> p c t i", i=2))
            y_words = keep.tile([P, width], U32, name="y_words%d" % c, align_bytes=64)
            nc.vector.quantize_mx(y_words[:].bitcast(FP8X4), y_scales[:, cols], y_bf[:].rearrange("p c t -> p (c t)"))
            nc.sync.dma_start(out_words[:, cols], y_words[:].bitcast(I32))
        for q in range(4):
            queue = nc.sync if q % 2 == 0 else nc.scalar
            queue.dma_start(
                out_2[0, 4 * q : 4 * q + 4, :].bitcast(I32), y_scales[32 * q : 32 * q + 4, :].bitcast(I32)
            )
